import numpy as np
import ml_dtypes


def mxq(x, axis, fmt="e4m3"):
    dtype, down = {"e4m3": (ml_dtypes.float8_e4m3fn, 7), "e5m2": (ml_dtypes.float8_e5m2, 14)}[fmt]
    v = np.moveaxis(np.asarray(x, np.float32).astype(ml_dtypes.bfloat16).astype(np.float64), axis, -1)
    blocks = v.reshape(v.shape[:-1] + (-1, 32))
    amax = np.abs(blocks).max(-1, keepdims=True)
    byte = np.maximum(np.where(amax > 0, np.frexp(amax)[1] - 1 + 127, 0) - down, 1)
    scale = np.exp2(byte - 127.0)
    codes = (blocks / scale).astype(np.float32).astype(dtype).astype(np.float64)
    return np.moveaxis((codes * scale).reshape(v.shape), -1, axis)


WIDE = False


def mx_kscale(k):
    if not WIDE:
        return np.ones(k)
    levels = np.array([10, -10, 5, -5, 0])
    if k % 512:
        return np.exp2(np.random.permutation(np.resize(levels, k // 32))).repeat(32)
    a = np.empty((k // 512, 16))
    for p in range(k // 512):
        a[p, :8] = np.random.permutation(np.resize(levels, 8))
        for g in range(8):
            far = levels[np.abs(levels - a[p, g]) >= 10]
            a[p, g + 8] = far[np.random.randint(len(far))]
    return np.exp2(a.ravel()).repeat(32)


BF16 = ml_dtypes.bfloat16


def bf(x):
    return np.asarray(x, np.float32).astype(BF16)


def f64(x):
    return np.asarray(x).astype(np.float64)


E2M1 = np.array([0.0, 0.5, 1.0, 1.5, 2.0, 3.0, 4.0, 6.0, -0.0, -0.5, -1.0, -1.5, -2.0, -3.0, -4.0, -6.0])


def pack_weight(w, fmt):
    k, n = w.shape
    w = f64(bf(w)).reshape(k // 32, 32, n)
    amax = np.abs(w).max(1)
    if fmt == "e4m3":
        byte = np.frexp(amax)[1] - 1 + 127 - 7
    else:
        mant, ex = np.frexp(amax / 6.0)
        byte = np.where(mant > 0.5, ex, ex - 1) + 127
    byte = np.clip(np.where(amax > 0, byte, 1), 1, 254)
    scaled = (w * np.exp2(127.0 - byte)[:, None, :]).reshape(k, n).astype(np.float32)
    by_word = np.ascontiguousarray(scaled.reshape(k // 512, 128, 4, n).transpose(0, 1, 3, 2))
    if fmt == "e4m3":
        words = by_word.astype(ml_dtypes.float8_e4m3fn).view(np.uint8)
    else:
        c = by_word.astype(ml_dtypes.float4_e2m1fn).view(np.uint8) & 0xF
        words = c[..., 0::2] | (c[..., 1::2] << 4)
    return np.ascontiguousarray(words), np.ascontiguousarray(byte.astype(np.uint8).reshape(k // 512, 16, n))


def unpack_weight(words, scales, fmt):
    g, p, n, _ = words.shape
    if fmt == "e4m3":
        vals = np.ascontiguousarray(words).view(ml_dtypes.float8_e4m3fn).astype(np.float64)
    else:
        nib = np.empty((g, p, n, 4), np.uint8)
        nib[..., 0::2] = words & 0xF
        nib[..., 1::2] = words >> 4
        vals = E2M1[nib]
    vals = vals * np.repeat(np.exp2(scales.astype(np.float64) - 127.0), 8, axis=1)[..., None]
    return vals.transpose(0, 1, 3, 2).reshape(g * 512, n)

E4M3FN = np.array([(-1.0 if i & 128 else 1.0) * ((1.0 + (i & 7) / 8.0) * 2.0 ** (((i >> 3) & 15) - 7) if i & 120 else (i & 7) * 2.0 ** -9) for i in range(256)])


def e4m3fn_bytes(y):
    return np.clip(np.asarray(y, np.float64), -448.0, 448.0).astype(np.float32).astype(ml_dtypes.float8_e4m3fn).view(np.uint8)


def e4m3fn_values(b):
    return E4M3FN[b]


N, D, F, R = 1024, 1024, 2048, 512


def draw0():
    s1, s2, t = mx_kscale(R), mx_kscale(R), mx_kscale(D)
    x = bf(np.random.standard_normal((N, D)) * t)
    a1_words, a1_scales = pack_weight((np.random.standard_normal((D, R)) / np.sqrt(D) * s1[None, :] / t[:, None]).T, "e4m3")
    b1_words, b1_scales = pack_weight((np.random.standard_normal((F, R)) / np.sqrt(R) / s1[None, :]).T, "e4m3")
    a2_words, a2_scales = pack_weight((np.random.standard_normal((D, R)) * s2[None, :]).T, "e4m3")
    b2_words, b2_scales = pack_weight((np.random.standard_normal((F, R)) / np.sqrt(R) / s2[None, :]).T, "e4m3")
    return {
        "x": x,
        "a1_words": a1_words,
        "a1_scales": a1_scales,
        "b1_words": b1_words,
        "b1_scales": b1_scales,
        "a2_words": a2_words,
        "a2_scales": a2_scales,
        "b2_words": b2_words,
        "b2_scales": b2_scales,
        "bias": bf(np.random.standard_normal(F) * 0.3),
    }


def low_rank(a_words, a_scales, b_words, b_scales):
    return unpack_weight(a_words, a_scales, "e4m3").T @ unpack_weight(b_words, b_scales, "e4m3")


def core(x, a1_words, a1_scales, b1_words, b1_scales, a2_words, a2_scales, b2_words, b2_scales, bias):
    w1 = low_rank(a1_words, a1_scales, b1_words, b1_scales)
    w2 = low_rank(a2_words, a2_scales, b2_words, b2_scales)
    w = w1 * (w2 + 1.0)
    h = (mxq(f64(x), 1, "e4m3") @ mxq(w, 0, "e4m3")) + f64(bias)[None, :]
    r = np.maximum(h, 0.0)
    return r * r


def setup_inputs():
    drawn = draw0()
    full = np.asarray(drawn['x']).astype(np.float64)
    scale = (np.abs(full).reshape(8, 128, 8, 128).max(axis=(1, 3)) / 448.0).astype(np.float32)
    given = {}
    for key, value in drawn.items():
        if key == 'x':
            given['x_bytes'] = e4m3fn_bytes(full / np.repeat(np.repeat(scale.astype(np.float64), 128, axis=0), 128, axis=1))
            given['x_scale'] = scale
        else:
            given[key] = value
    return given


def reference(x_bytes, x_scale, a1_words, a1_scales, b1_words, b1_scales, a2_words, a2_scales, b2_words, b2_scales, bias):
    return core(e4m3fn_values(x_bytes) * np.repeat(np.repeat(x_scale.astype(np.float64), 128, axis=0), 128, axis=1), a1_words, a1_scales, b1_words, b1_scales, a2_words, a2_scales, b2_words, b2_scales, bias)

@@ -1,0 +1,317 @@
+from contextlib import ExitStack
+
+import concourse.mybir as mybir
+from concourse.masks import make_identity
+
+N, D, F, R = 1024, 1024, 2048, 512
+FLOPS = 2 * (2 * D * F * R) + 2 * N * D * F
+
+F32 = mybir.dt.float32
+BF16 = mybir.dt.bfloat16
+I32 = mybir.dt.int32
+U32 = mybir.dt.uint32
+U8 = mybir.dt.uint8
+FP8 = mybir.dt.float8_e4m3fn
+FP8X4 = mybir.dt.float8_e4m3fn_x4
+ALU = mybir.AluOpType
+ACT = mybir.ActivationFunctionType
+
+P = 128
+PACK = 4
+K_PASS = P * PACK
+PASSES = D // K_PASS
+CHUNK = 512
+CHUNKS = F // CHUNK
+SUBS = CHUNK // P
+TILES = N // P
+W_UNITS = CHUNKS * PASSES * SUBS
+H_UNITS = CHUNKS * TILES
+H_LAG = 12
+SQ_LAG = 17
+POOL_UNITS = 30
+F32_MAX = 3.4028234663852886e38
+
+
+def tile_personalizedfedparasquaredrelu_d2p_kernel(
+    tc, x_bytes, x_scale, a1_words, a1_scales, b1_words, b1_scales,
+    a2_words, a2_scales, b2_words, b2_scales, bias, out,
+):
+    nc = tc.nc
+    a_words, a_scales = (a1_words, a2_words), (a1_scales, a2_scales)
+    b_words, b_scales = (b1_words, b2_words), (b1_scales, b2_scales)
+
+    with ExitStack() as ctx:
+        keep = ctx.enter_context(tc.tile_pool(name="keep", bufs=1))
+        work = ctx.enter_context(tc.tile_pool(name="work", bufs=3))
+        psum = ctx.enter_context(tc.psum_pool(name="psum", bufs=3))
+        ctx.enter_context(tc.manual_schedule())
+
+        def kept(name, shape, dtype):
+            return keep.tile(shape, dtype, name=name, align_bytes=64)
+
+        ident = kept("ident", [P, P], F32)
+        sel = kept("sel", [P, CHUNKS], BF16)
+        bias_rows = kept("bias_rows", [P, CHUNK], BF16)
+        bias_all = kept("bias_all", [P, F], BF16)
+        xs_all = kept("xs_all", [P, TILES * TILES], F32)
+        x_raw = [kept("x_raw%d" % k, [P, 2, D], U8) for k in range(TILES // 2)]
+        a_raw = {(w, g): kept("a_raw%d%d" % (w, g), [P, K_PASS], U32) for w in range(2) for g in range(PASSES)}
+        a_codes = {(w, g): kept("a_codes%d%d" % (w, g), [P, K_PASS], U32) for w in range(2) for g in range(PASSES)}
+        asc_raw = kept("asc_raw", [P, K_PASS], U8)
+        asc = kept("asc", [P, K_PASS], U8)
+        bsc = kept("bsc", [P, F], U8)
+        b_codes = {(w, c): kept("b_codes%d%d" % (w, c), [P, CHUNK], U32) for w in range(2) for c in range(CHUNKS)}
+        x_codes = [kept("x_codes%d" % k, [P, 2 * PASSES * P], U32) for k in range(TILES // 2)]
+        x_sc = [kept("x_sc%d" % k, [P, 2 * PASSES * P], U8) for k in range(TILES // 2)]
+        w_codes = [kept("w_codes%d" % q, [P, CHUNK], U32) for q in range(CHUNKS * PASSES)]
+        w_sc = [kept("w_sc%d" % q, [P, CHUNK], U8) for q in range(CHUNKS * PASSES)]
+
+        def load_x(k):
+            nc.sync.dma_start(out=x_raw[k][:], in_=x_bytes[256 * k : 256 * (k + 1), :].rearrange("(i p) d -> p i d", p=P))
+
+        def load_a(w, g):
+            src = a_words[w][0].rearrange("p n t -> p (n t)")[:, 2048 * g : 2048 * (g + 1)].bitcast(I32)
+            nc.sync.dma_start(out=a_raw[w, g][:].bitcast(I32), in_=src)
+
+        def load_b(w, c):
+            src = b_words[w][0].rearrange("p n t -> p (n t)")[:, 2048 * c : 2048 * (c + 1)].bitcast(I32)
+            nc.sync.dma_start(out=b_codes[w, c][:].bitcast(I32), in_=src)
+
+        def load_asc(w):
+            for q in range(4):
+                src = a_scales[w][0, 4 * q : 4 * q + 4, :].bitcast(I32).rearrange("r (g n) -> g r n", g=PASSES)
+                row = 32 * q + 8 * w
+                nc.sync.dma_start(out=asc_raw[row : row + 8, :].bitcast(I32), in_=src)
+
+        def load_bsc(w, queue):
+            for q in range(4):
+                row = 32 * q + 4 + 4 * w
+                queue.dma_start(out=bsc[row : row + 4, :].bitcast(I32), in_=b_scales[w][0, 4 * q : 4 * q + 4, :].bitcast(I32))
+
+        nc.vector.memset(asc_raw[:].bitcast(I32), 0)
+        nc.vector.memset(bsc[:].bitcast(I32), 0)
+        nc.vector.memset(bias_rows[:].bitcast(I32), 0)
+        make_identity(nc, ident[:])
+        nc.scalar.activation(out=sel[:], in_=ident[:, 0:CHUNKS], func=ACT.Square)
+
+        nc.sync.dma_start(out=xs_all[:], in_=x_scale.rearrange("i j -> (i j)").partition_broadcast(P))
+        load_x(0)
+        load_bsc(0, nc.gpsimd)
+        load_asc(1)
+        load_asc(0)
+        load_x(1)
+        load_a(1, 0)
+        load_a(0, 0)
+        load_bsc(1, nc.sync)
+        load_b(1, 0)
+        load_b(0, 0)
+        load_a(1, 1)
+        load_a(0, 1)
+        load_x(2)
+        nc.sync.dma_start(out=bias_rows[0:CHUNKS, :], in_=bias.rearrange("(c n) -> c n", n=CHUNK))
+        load_x(3)
+        for c in range(1, CHUNKS):
+            load_b(1, c)
+            load_b(0, c)
+
+        x_wide, x_banks, x_turned = {}, {}, {}
+        w2_sb, w1_banks, w_bf, h_banks, s_pairs, r_pairs = {}, {}, {}, {}, {}, {}
+
+        def widen(i, on_vector, blocks):
+            if i not in x_wide:
+                x_wide[i] = work.tile([P, D], BF16, name="x_wide", align_bytes=64, bufs=4)
+            for j in blocks:
+                cols = slice(P * j, P * (j + 1))
+                src = x_raw[i // 2][:, i % 2, cols].bitcast(FP8)
+                scale = xs_all[:, TILES * i + j : TILES * i + j + 1]
+                if on_vector:
+                    nc.vector.tensor_scalar(out=x_wide[i][:, cols], in0=src, scalar1=scale, scalar2=None, op0=ALU.mult)
+                else:
+                    nc.scalar.activation(out=x_wide[i][:, cols], in_=src, func=ACT.Copy, scale=scale)
+
+        def turn(i):
+            x_banks[i] = psum.tile([P, PASSES, 2, P], F32, name="x_bank", tag="h")
+            words = x_wide[i][:].bitcast(F32)
+            for g in range(PASSES):
+                for u in range(2):
+                    nc.tensor.transpose(x_banks[i][:, g, u, :], words[:, 256 * g + u : 256 * (g + 1) : 2], ident[:])
+
+        def empty_x(i):
+            k = i // 2
+            if k not in x_turned:
+                x_turned[k] = work.tile([P, 2, PASSES * P * 2], F32, name="x_turned", align_bytes=64, bufs=2)
+            nc.scalar.copy(
+                out=x_turned[k][:, i % 2, :].rearrange("p (g n u) -> p g n u", g=PASSES, u=2),
+                in_=x_banks[i][:].rearrange("p g u n -> p g n u"),
+            )
+
+        def quantize_x(k):
+            nc.vector.quantize_mx(
+                out=x_codes[k][:].bitcast(FP8X4), scales=x_sc[k][:],
+                in_=x_turned[k][:].rearrange("p i n -> p (i n)").bitcast(BF16),
+            )
+
+        def permute_a(w, g):
+            nc.vector.tensor_copy(
+                out=a_codes[w, g][:].bitcast(I32).rearrange("p (t b i) -> p b t i", t=PACK, i=4),
+                in_=a_raw[w, g][:].bitcast(I32).rearrange("p (b i t) -> p b t i", t=PACK, i=4),
+            )
+
+        def permute_asc():
+            nc.vector.tensor_copy(
+                out=asc[:].rearrange("p (t m) -> p t m", t=PACK),
+                in_=asc_raw[:].rearrange("p (m t) -> p t m", t=PACK),
+            )
+
+        def spread_bias(half):
+            bank = psum.tile([P, 2 * CHUNK], BF16, name="bias_bank", tag="h")
+            for e in range(2):
+                c = 2 * half + e
+                nc.tensor.matmul(
+                    bank[:, CHUNK * e : CHUNK * (e + 1)], lhsT=sel[:, c : c + 1].to_broadcast([P, P]),
+                    rhs=bias_rows[:], start=True, stop=True,
+                )
+            nc.scalar.copy(out=bias_all[:, 2 * CHUNK * half : 2 * CHUNK * (half + 1)], in_=bank[:])
+
+        def factor_product(w, u, bank):
+            c, g, s = u // (PASSES * SUBS), u // SUBS % PASSES, u % SUBS
+            a_row, b_row = 8 * w + 4 * g, 4 + 4 * w
+            for t in range(PACK):
+                nc.tensor.matmul_mx(
+                    out=bank[:, t, :],
+                    lhsT=a_codes[w, g][:, P * t : P * (t + 1)].bitcast(FP8X4),
+                    lhsT_scale=asc[a_row:P, P * t : P * (t + 1)],
+                    rhs=b_codes[w, c][:, P * s : P * (s + 1)].bitcast(FP8X4),
+                    rhs_scale=bsc[b_row:P, CHUNK * c + P * s : CHUNK * c + P * (s + 1)],
+                    start=True, stop=True,
+                )
+
+        def w_products(u):
+            w2_bank = psum.tile([P, PACK, P], F32, name="w2_bank", tag="w2", bufs=2)
+            factor_product(1, u, w2_bank)
+            w1_banks[u] = psum.tile([P, PACK, P], F32, name="w1_bank", tag="w1")
+            factor_product(0, u, w1_banks[u])
+            w2_sb[u] = work.tile([P, P, PACK], F32, name="w2_sb", align_bytes=64)
+            nc.scalar.copy(out=w2_sb[u][:], in_=w2_bank[:].rearrange("p t n -> p n t"))
+
+        def w_combine(u):
+            q, s = u // SUBS, u % SUBS
+            if s == 0:
+                w_bf[q] = work.tile([P, CHUNK, PACK], BF16, name="w_bf", align_bytes=64)
+            nc.vector.scalar_tensor_tensor(
+                out=w_bf[q][:, P * s : P * (s + 1), :], in0=w2_sb[u][:], scalar=1.0,
+                in1=w1_banks[u][:].rearrange("p t n -> p n t"), op0=ALU.add, op1=ALU.mult,
+            )
+
+        def quantize_w(q):
+            nc.vector.quantize_mx(
+                out=w_codes[q][:].bitcast(FP8X4), scales=w_sc[q][:], in_=w_bf[q][:].rearrange("p n t -> p (n t)"),
+            )
+
+        def h_product(v):
+            c, i = v // TILES, v % TILES
+            h_banks[v] = psum.tile([P, CHUNK], F32, name="h_bank", tag="h")
+            for g in range(PASSES):
+                cols = slice(P * (PASSES * (i % 2) + g), P * (PASSES * (i % 2) + g + 1))
+                nc.tensor.matmul_mx(
+                    out=h_banks[v][:],
+                    lhsT=x_codes[i // 2][:, cols].bitcast(FP8X4), lhsT_scale=x_sc[i // 2][:, cols],
+                    rhs=w_codes[PASSES * c + g][:].bitcast(FP8X4), rhs_scale=w_sc[PASSES * c + g][:],
+                    start=(g == 0), stop=(g == PASSES - 1),
+                )
+
+        def add_bias(v):
+            c = v // TILES
+            if v % 2 == 0:
+                s_pairs[v // 2] = work.tile([P, 2, CHUNK], F32, name="s_pair", align_bytes=64)
+            nc.vector.tensor_tensor(
+                out=s_pairs[v // 2][:, v % 2, :], in0=h_banks[v][:],
+                in1=bias_all[:, CHUNK * c : CHUNK * (c + 1)], op=ALU.add,
+            )
+
+        def relu_pair(k):
+            r_pairs[k] = work.tile([P, 2, CHUNK], F32, name="r_pair", align_bytes=64, bufs=4)
+            nc.gpsimd.tensor_scalar(out=r_pairs[k][:], in0=s_pairs[k][:], scalar1=F32_MAX, scalar2=0.0, op0=ALU.min, op1=ALU.max)
+
+        def store(v, res):
+            c, i = v // TILES, v % TILES
+            nc.sync.dma_start(out=out[P * i : P * (i + 1), CHUNK * c : CHUNK * (c + 1)], in_=res[:])
+
+        def square(v):
+            res = work.tile([P, CHUNK], F32, name="res", align_bytes=64, bufs=6)
+            nc.scalar.activation(out=res[:], in_=r_pairs[v // 2][:, v % 2, :], func=ACT.Square)
+            store(v, res)
+
+        def relu_square(v):
+            res = work.tile([P, CHUNK], F32, name="res", align_bytes=64, bufs=6)
+            s = s_pairs[v // 2][:, v % 2, :]
+            nc.vector.scalar_tensor_tensor(out=res[:], in0=s, scalar=0.0, in1=s, op0=ALU.max, op1=ALU.mult)
+            store(v, res)
+
+        first, second, whole = range(0, 4), range(4, 8), range(8)
+        widen(0, True, whole)
+        widen(1, False, whole)
+        turn(0)
+        turn(1)
+        empty_x(0)
+        empty_x(1)
+        widen(2, True, whole)
+        permute_asc()
+        permute_a(1, 0)
+        permute_a(0, 0)
+        widen(3, False, whole)
+        turn(2)
+        turn(3)
+        quantize_x(0)
+        empty_x(2)
+
+        for m in range(H_UNITS + SQ_LAG):
+            if m < W_UNITS:
+                w_products(m)
+            if m == 0:
+                empty_x(3)
+                permute_a(1, 1)
+                permute_a(0, 1)
+            if m == 1:
+                widen(4, False, first)
+            if m == 2:
+                widen(4, False, second)
+                widen(5, True, whole)
+            if m == 3:
+                turn(4)
+                turn(5)
+                empty_x(4)
+            if m == 4:
+                empty_x(5)
+            if m == 5:
+                spread_bias(0)
+            if m == 6:
+                spread_bias(1)
+                widen(6, True, whole)
+            if m == 7:
+                widen(7, False, first)
+            if m == 8:
+                widen(7, False, second)
+            if m == 9:
+                turn(6)
+                turn(7)
+                empty_x(6)
+            if m == 10:
+                empty_x(7)
+            v = m - H_LAG
+            if 0 <= v < H_UNITS:
+                h_product(v)
+            if m < W_UNITS:
+                w_combine(m)
+            if m % SUBS == 1 and 0 <= m // SUBS - 1 < CHUNKS * PASSES:
+                quantize_w(m // SUBS - 1)
+            if m in (3, 7, 11):
+                quantize_x(m // 4 + 1)
+            if 0 <= v < H_UNITS:
+                add_bias(v)
+                if v % 2 == 1 and v < POOL_UNITS:
+                    relu_pair(v // 2)
+            if 0 <= m - SQ_LAG < POOL_UNITS:
+                square(m - SQ_LAG)
+        for last in range(POOL_UNITS, H_UNITS):
+            relu_square(last)

@@ -27,8 +27,19 @@ TILES = N // P
 W_UNITS = CHUNKS * PASSES * SUBS
 H_UNITS = CHUNKS * TILES
 H_LAG = 12
-SQ_LAG = 17
-POOL_UNITS = 30
+SQ_LAG = 16
+POOL_UNITS = 28
+ACT_PAIRS = (9,)
+POOL_SQ = ()
+DVE_WIDEN = (5, 7, 6)
+WARM = 1
+PERM_POOL = 0
+X_FIRST = 1
+NA = 1
+NB = 3
+ORDER = [('warm', 4), ('wv', 0, 0), ('wv', 0, 1), ('wa', 1, 0), ('wa', 1, 1), ('wv', 2, 0), ('wv', 2, 1), ('wv', 3, 0), ('wv', 3, 1), ('t', 0, 'h'), ('t', 1, 'h'), ('warm', 2), ('e', 0), ('e', 1), ('t', 2, 'h'), ('t', 3, 'w1'), ('warm', 2), ('ps',), ('pa', 1, 0), ('pa', 0, 0), ('e', 2), ('e', 3), ('wv', 4, 0), ('wv', 4, 1), ('wv', 5, 0), ('wv', 5, 1), ('q', 0), ('F', 0), ('q', 1), ('B', 0), ('F', 1), ('pa', 1, 1), ('t', 4, 'h'), ('t', 5, 'h'), ('e', 4), ('B', 1), ('F', 2), ('pa', 0, 1), ('wv', 6, 0), ('wv', 6, 1), ('B', 2), ('F', 3), ('e', 5), ('wv', 7, 0), ('wv', 7, 1), ('B', 3), ('F', 4), ('B', 4), ('F', 5), ('q', 2), ('t', 6, 'h'), ('t', 7, 'h'), ('e', 6), ('B', 5), ('F', 6), ('B', 6), ('F', 7), ('e', 7), ('bias', 0), ('B', 7), ('F', 8), ('B', 8), ('F', 9), ('q', 3), ('B', 9), ('F', 10), ('bias', 1), ('B', 10), ('F', 11), ('B', 11), ('F', 12), ('B', 12), ('F', 13), ('B', 13), ('F', 14), ('B', 14), ('F', 15), ('B', 15), ('F', 16), ('B', 16), ('F', 17), ('B', 17), ('F', 18), ('B', 18), ('F', 19), ('B', 19)]
+TAIL_LAG = 14
+BANKS = {"h": 3, "w1": 3, "w2": 2}
 F32_MAX = 3.4028234663852886e38
 
 
@@ -54,7 +65,7 @@ def tile_personalizedfedparasquaredrelu_d2p_kernel(
         bias_rows = kept("bias_rows", [P, CHUNK], BF16)
         bias_all = kept("bias_all", [P, F], BF16)
         xs_all = kept("xs_all", [P, TILES * TILES], F32)
-        x_raw = [kept("x_raw%d" % k, [P, 2, D], U8) for k in range(TILES // 2)]
+        x_raw = [kept("x_raw%d" % k, [P, 4, D], U8) for k in range(TILES // 4)]
         a_raw = {(w, g): kept("a_raw%d%d" % (w, g), [P, K_PASS], U32) for w in range(2) for g in range(PASSES)}
         a_codes = {(w, g): kept("a_codes%d%d" % (w, g), [P, K_PASS], U32) for w in range(2) for g in range(PASSES)}
         asc_raw = kept("asc_raw", [P, K_PASS], U8)
@@ -67,7 +78,7 @@ def tile_personalizedfedparasquaredrelu_d2p_kernel(
         w_sc = [kept("w_sc%d" % q, [P, CHUNK], U8) for q in range(CHUNKS * PASSES)]
 
         def load_x(k):
-            nc.sync.dma_start(out=x_raw[k][:], in_=x_bytes[256 * k : 256 * (k + 1), :].rearrange("(i p) d -> p i d", p=P))
+            nc.sync.dma_start(out=x_raw[k][:], in_=x_bytes[512 * k : 512 * (k + 1), :].rearrange("(i p) d -> p i d", p=P))
 
         def load_a(w, g):
             src = a_words[w][0].rearrange("p n t -> p (n t)")[:, 2048 * g : 2048 * (g + 1)].bitcast(I32)
@@ -77,14 +88,14 @@ def tile_personalizedfedparasquaredrelu_d2p_kernel(
             src = b_words[w][0].rearrange("p n t -> p (n t)")[:, 2048 * c : 2048 * (c + 1)].bitcast(I32)
             nc.sync.dma_start(out=b_codes[w, c][:].bitcast(I32), in_=src)
 
-        def load_asc(w):
-            for q in range(4):
+        def load_asc(w, quads, queue):
+            for q in quads:
                 src = a_scales[w][0, 4 * q : 4 * q + 4, :].bitcast(I32).rearrange("r (g n) -> g r n", g=PASSES)
                 row = 32 * q + 8 * w
-                nc.sync.dma_start(out=asc_raw[row : row + 8, :].bitcast(I32), in_=src)
+                queue.dma_start(out=asc_raw[row : row + 8, :].bitcast(I32), in_=src)
 
-        def load_bsc(w, queue):
-            for q in range(4):
+        def load_bsc(w, quads, queue):
+            for q in quads:
                 row = 32 * q + 4 + 4 * w
                 queue.dma_start(out=bsc[row : row + 4, :].bitcast(I32), in_=b_scales[w][0, 4 * q : 4 * q + 4, :].bitcast(I32))
 
@@ -92,24 +103,27 @@ def tile_personalizedfedparasquaredrelu_d2p_kernel(
         nc.vector.memset(bsc[:].bitcast(I32), 0)
         nc.vector.memset(bias_rows[:].bitcast(I32), 0)
         make_identity(nc, ident[:])
+        load_asc(0, range(NA, 4), nc.gpsimd)
+        load_bsc(0, range(NB), nc.gpsimd)
         nc.scalar.activation(out=sel[:], in_=ident[:, 0:CHUNKS], func=ACT.Square)
 
         nc.sync.dma_start(out=xs_all[:], in_=x_scale.rearrange("i j -> (i j)").partition_broadcast(P))
         load_x(0)
-        load_bsc(0, nc.gpsimd)
-        load_asc(1)
-        load_asc(0)
-        load_x(1)
+        if X_FIRST:
+            load_x(1)
+        load_asc(1, range(4), nc.sync)
+        load_asc(0, range(NA), nc.sync)
         load_a(1, 0)
         load_a(0, 0)
-        load_bsc(1, nc.sync)
         load_b(1, 0)
+        load_bsc(1, range(4), nc.sync)
         load_b(0, 0)
+        load_bsc(0, range(NB, 4), nc.sync)
+        if not X_FIRST:
+            load_x(1)
         load_a(1, 1)
         load_a(0, 1)
-        load_x(2)
         nc.sync.dma_start(out=bias_rows[0:CHUNKS, :], in_=bias.rearrange("(c n) -> c n", n=CHUNK))
-        load_x(3)
         for c in range(1, CHUNKS):
             load_b(1, c)
             load_b(0, c)
@@ -119,18 +133,18 @@ def tile_personalizedfedparasquaredrelu_d2p_kernel(
 
         def widen(i, on_vector, blocks):
             if i not in x_wide:
-                x_wide[i] = work.tile([P, D], BF16, name="x_wide", align_bytes=64, bufs=4)
+                x_wide[i] = work.tile([P, D], BF16, name="x_wide", align_bytes=64, bufs=8)
             for j in blocks:
                 cols = slice(P * j, P * (j + 1))
-                src = x_raw[i // 2][:, i % 2, cols].bitcast(FP8)
+                src = x_raw[i // 4][:, i % 4, cols].bitcast(FP8)
                 scale = xs_all[:, TILES * i + j : TILES * i + j + 1]
                 if on_vector:
                     nc.vector.tensor_scalar(out=x_wide[i][:, cols], in0=src, scalar1=scale, scalar2=None, op0=ALU.mult)
                 else:
                     nc.scalar.activation(out=x_wide[i][:, cols], in_=src, func=ACT.Copy, scale=scale)
 
-        def turn(i):
-            x_banks[i] = psum.tile([P, PASSES, 2, P], F32, name="x_bank", tag="h")
+        def turn(i, tag):
+            x_banks[i] = psum.tile([P, PASSES, 2, P], F32, name="x_bank", tag=tag, bufs=BANKS[tag])
             words = x_wide[i][:].bitcast(F32)
             for g in range(PASSES):
                 for u in range(2):
@@ -139,7 +153,7 @@ def tile_personalizedfedparasquaredrelu_d2p_kernel(
         def empty_x(i):
             k = i // 2
             if k not in x_turned:
-                x_turned[k] = work.tile([P, 2, PASSES * P * 2], F32, name="x_turned", align_bytes=64, bufs=2)
+                x_turned[k] = work.tile([P, 2, PASSES * P * 2], F32, name="x_turned", align_bytes=64, bufs=4)
             nc.scalar.copy(
                 out=x_turned[k][:, i % 2, :].rearrange("p (g n u) -> p g n u", g=PASSES, u=2),
                 in_=x_banks[i][:].rearrange("p g u n -> p g n u"),
@@ -152,7 +166,7 @@ def tile_personalizedfedparasquaredrelu_d2p_kernel(
             )
 
         def permute_a(w, g):
-            nc.vector.tensor_copy(
+            (nc.gpsimd if g and PERM_POOL else nc.vector).tensor_copy(
                 out=a_codes[w, g][:].bitcast(I32).rearrange("p (t b i) -> p b t i", t=PACK, i=4),
                 in_=a_raw[w, g][:].bitcast(I32).rearrange("p (b i t) -> p b t i", t=PACK, i=4),
             )
@@ -210,7 +224,8 @@ def tile_personalizedfedparasquaredrelu_d2p_kernel(
 
         def h_product(v):
             c, i = v // TILES, v % TILES
-            h_banks[v] = psum.tile([P, CHUNK], F32, name="h_bank", tag="h")
+            tag = "w1" if v > W_UNITS - H_LAG and v % 2 == 0 else "h"
+            h_banks[v] = psum.tile([P, CHUNK], F32, name="h_bank", tag=tag)
             for g in range(PASSES):
                 cols = slice(P * (PASSES * (i % 2) + g), P * (PASSES * (i % 2) + g + 1))
                 nc.tensor.matmul_mx(
@@ -223,14 +238,20 @@ def tile_personalizedfedparasquaredrelu_d2p_kernel(
         def add_bias(v):
             c = v // TILES
             if v % 2 == 0:
-                s_pairs[v // 2] = work.tile([P, 2, CHUNK], F32, name="s_pair", align_bytes=64)
+                s_pairs[v // 2] = work.tile([P, 2, CHUNK], F32, name="s_pair", align_bytes=64, bufs=5)
             nc.vector.tensor_tensor(
                 out=s_pairs[v // 2][:, v % 2, :], in0=h_banks[v][:],
                 in1=bias_all[:, CHUNK * c : CHUNK * (c + 1)], op=ALU.add,
             )
 
         def relu_pair(k):
-            r_pairs[k] = work.tile([P, 2, CHUNK], F32, name="r_pair", align_bytes=64, bufs=4)
+            r_pairs[k] = work.tile([P, 2, CHUNK], F32, name="r_pair", align_bytes=64, bufs=5)
+            if k in ACT_PAIRS:
+                for e in range(2):
+                    nc.scalar.activation(out=r_pairs[k][:, e, :], in_=s_pairs[k][:, e, :], func=ACT.Relu)
+                for e in range(2):
+                    square(2 * k + e)
+                return
             nc.gpsimd.tensor_scalar(out=r_pairs[k][:], in0=s_pairs[k][:], scalar1=F32_MAX, scalar2=0.0, op0=ALU.min, op1=ALU.max)
 
         def store(v, res):
@@ -238,80 +259,67 @@ def tile_personalizedfedparasquaredrelu_d2p_kernel(
             nc.sync.dma_start(out=out[P * i : P * (i + 1), CHUNK * c : CHUNK * (c + 1)], in_=res[:])
 
         def square(v):
-            res = work.tile([P, CHUNK], F32, name="res", align_bytes=64, bufs=6)
-            nc.scalar.activation(out=res[:], in_=r_pairs[v // 2][:, v % 2, :], func=ACT.Square)
+            res = work.tile([P, CHUNK], F32, name="res", align_bytes=64, bufs=12)
+            r = r_pairs[v // 2][:, v % 2, :]
+            if v in POOL_SQ:
+                nc.gpsimd.tensor_tensor(out=res[:], in0=r, in1=r, op=ALU.mult)
+            else:
+                nc.scalar.activation(out=res[:], in_=r, func=ACT.Square)
             store(v, res)
 
         def relu_square(v):
-            res = work.tile([P, CHUNK], F32, name="res", align_bytes=64, bufs=6)
+            res = work.tile([P, CHUNK], F32, name="res", align_bytes=64, bufs=12)
             s = s_pairs[v // 2][:, v % 2, :]
             nc.vector.scalar_tensor_tensor(out=res[:], in0=s, scalar=0.0, in1=s, op0=ALU.max, op1=ALU.mult)
             store(v, res)
 
-        first, second, whole = range(0, 4), range(4, 8), range(8)
-        widen(0, True, whole)
-        widen(1, False, whole)
-        turn(0)
-        turn(1)
-        empty_x(0)
-        empty_x(1)
-        widen(2, True, whole)
-        permute_asc()
-        permute_a(1, 0)
-        permute_a(0, 0)
-        widen(3, False, whole)
-        turn(2)
-        turn(3)
-        quantize_x(0)
-        empty_x(2)
+        warm_bank = psum.tile([P, P], F32, name="warm_bank", tag="w1")
 
-        for m in range(H_UNITS + SQ_LAG):
-            if m < W_UNITS:
+        def warm(count):
+            for k in range(count * WARM):
+                nc.tensor.matmul(warm_bank[:], lhsT=ident[:], rhs=ident[:], start=True, stop=True)
+
+        last = W_UNITS - 1
+        state = {"done": 0}
+
+        def front(m):
+            if m < last:
                 w_products(m)
-            if m == 0:
-                empty_x(3)
-                permute_a(1, 1)
-                permute_a(0, 1)
-            if m == 1:
-                widen(4, False, first)
-            if m == 2:
-                widen(4, False, second)
-                widen(5, True, whole)
-            if m == 3:
-                turn(4)
-                turn(5)
-                empty_x(4)
-            if m == 4:
-                empty_x(5)
-            if m == 5:
-                spread_bias(0)
-            if m == 6:
-                spread_bias(1)
-                widen(6, True, whole)
-            if m == 7:
-                widen(7, False, first)
-            if m == 8:
-                widen(7, False, second)
-            if m == 9:
-                turn(6)
-                turn(7)
-                empty_x(6)
-            if m == 10:
-                empty_x(7)
             v = m - H_LAG
             if 0 <= v < H_UNITS:
                 h_product(v)
-            if m < W_UNITS:
+
+        def back(m):
+            v = m - H_LAG
+            if m < last:
                 w_combine(m)
-            if m % SUBS == 1 and 0 <= m // SUBS - 1 < CHUNKS * PASSES:
+            if m == last - 1:
+                w_products(last)
+                w_combine(last)
+            if m % SUBS == 1 and 0 <= m // SUBS - 1 < CHUNKS * PASSES - 1:
                 quantize_w(m // SUBS - 1)
-            if m in (3, 7, 11):
-                quantize_x(m // 4 + 1)
+            if m == last:
+                quantize_w(CHUNKS * PASSES - 1)
             if 0 <= v < H_UNITS:
                 add_bias(v)
-                if v % 2 == 1 and v < POOL_UNITS:
-                    relu_pair(v // 2)
-            if 0 <= m - SQ_LAG < POOL_UNITS:
-                square(m - SQ_LAG)
-        for last in range(POOL_UNITS, H_UNITS):
-            relu_square(last)
+            lag = SQ_LAG if m < last else TAIL_LAG
+            while state["done"] < POOL_UNITS and state["done"] <= m - lag:
+                if state["done"] // 2 not in ACT_PAIRS:
+                    square(state["done"])
+                state["done"] += 1
+            if 0 <= v < POOL_UNITS and v % 2 == 1:
+                relu_pair(v // 2)
+
+        calls = {
+            "wv": lambda i, h: widen(i, True, range(4 * h, 4 * h + 4)),
+            "wa": lambda i, h: widen(i, False, range(4 * h, 4 * h + 4)),
+            "t": turn, "e": empty_x, "q": quantize_x, "pa": permute_a, "ps": permute_asc,
+            "warm": warm, "bias": spread_bias, "F": front, "B": back,
+        }
+        for job in ORDER:
+            calls[job[0]](*job[1:])
+        for m in range(20, H_UNITS + SQ_LAG):
+            front(m)
+            back(m)
+        for v in range(POOL_UNITS, H_UNITS):
+            relu_square(v)

from contextlib import ExitStack

import concourse.mybir as mybir
from concourse.masks import make_identity

N, D, F, R = 1024, 1024, 2048, 512
FLOPS = 2 * (2 * D * F * R) + 2 * N * D * F

F32 = mybir.dt.float32
BF16 = mybir.dt.bfloat16
I32 = mybir.dt.int32
U32 = mybir.dt.uint32
U8 = mybir.dt.uint8
FP8 = mybir.dt.float8_e4m3fn
FP8X4 = mybir.dt.float8_e4m3fn_x4
ALU = mybir.AluOpType
ACT = mybir.ActivationFunctionType

P = 128
PACK = 4
K_PASS = P * PACK
PASSES = D // K_PASS
CHUNK = 512
CHUNKS = F // CHUNK
SUBS = CHUNK // P
TILES = N // P
W_UNITS = CHUNKS * PASSES * SUBS
H_UNITS = CHUNKS * TILES
H_LAG = 12
SQ_LAG = 16
POOL_UNITS = 28
ACT_PAIRS = (9,)
POOL_SQ = ()
DVE_WIDEN = (5, 7, 6)
WARM = 1
PERM_POOL = 0
X_FIRST = 1
NA = 1
NB = 3
ORDER = [('warm', 4), ('wv', 0, 0), ('wv', 0, 1), ('wa', 1, 0), ('wa', 1, 1), ('wv', 2, 0), ('wv', 2, 1), ('wv', 3, 0), ('wv', 3, 1), ('t', 0, 'h'), ('t', 1, 'h'), ('warm', 2), ('e', 0), ('e', 1), ('t', 2, 'h'), ('t', 3, 'w1'), ('warm', 2), ('ps',), ('pa', 1, 0), ('pa', 0, 0), ('e', 2), ('e', 3), ('wv', 4, 0), ('wv', 4, 1), ('wv', 5, 0), ('wv', 5, 1), ('q', 0), ('F', 0), ('q', 1), ('B', 0), ('F', 1), ('pa', 1, 1), ('t', 4, 'h'), ('t', 5, 'h'), ('e', 4), ('B', 1), ('F', 2), ('pa', 0, 1), ('wv', 6, 0), ('wv', 6, 1), ('B', 2), ('F', 3), ('e', 5), ('wv', 7, 0), ('wv', 7, 1), ('B', 3), ('F', 4), ('B', 4), ('F', 5), ('q', 2), ('t', 6, 'h'), ('t', 7, 'h'), ('e', 6), ('B', 5), ('F', 6), ('B', 6), ('F', 7), ('e', 7), ('bias', 0), ('B', 7), ('F', 8), ('B', 8), ('F', 9), ('q', 3), ('B', 9), ('F', 10), ('bias', 1), ('B', 10), ('F', 11), ('B', 11), ('F', 12), ('B', 12), ('F', 13), ('B', 13), ('F', 14), ('B', 14), ('F', 15), ('B', 15), ('F', 16), ('B', 16), ('F', 17), ('B', 17), ('F', 18), ('B', 18), ('F', 19), ('B', 19)]
TAIL_LAG = 14
BANKS = {"h": 3, "w1": 3, "w2": 2}
F32_MAX = 3.4028234663852886e38


def tile_personalizedfedparasquaredrelu_d2p_kernel(
    tc, x_bytes, x_scale, a1_words, a1_scales, b1_words, b1_scales,
    a2_words, a2_scales, b2_words, b2_scales, bias, out,
):
    nc = tc.nc
    a_words, a_scales = (a1_words, a2_words), (a1_scales, a2_scales)
    b_words, b_scales = (b1_words, b2_words), (b1_scales, b2_scales)

    with ExitStack() as ctx:
        keep = ctx.enter_context(tc.tile_pool(name="keep", bufs=1))
        work = ctx.enter_context(tc.tile_pool(name="work", bufs=3))
        psum = ctx.enter_context(tc.psum_pool(name="psum", bufs=3))
        ctx.enter_context(tc.manual_schedule())

        def kept(name, shape, dtype):
            return keep.tile(shape, dtype, name=name, align_bytes=64)

        ident = kept("ident", [P, P], F32)
        sel = kept("sel", [P, CHUNKS], BF16)
        bias_rows = kept("bias_rows", [P, CHUNK], BF16)
        bias_all = kept("bias_all", [P, F], BF16)
        xs_all = kept("xs_all", [P, TILES * TILES], F32)
        x_raw = [kept("x_raw%d" % k, [P, 4, D], U8) for k in range(TILES // 4)]
        a_raw = {(w, g): kept("a_raw%d%d" % (w, g), [P, K_PASS], U32) for w in range(2) for g in range(PASSES)}
        a_codes = {(w, g): kept("a_codes%d%d" % (w, g), [P, K_PASS], U32) for w in range(2) for g in range(PASSES)}
        asc_raw = kept("asc_raw", [P, K_PASS], U8)
        asc = kept("asc", [P, K_PASS], U8)
        bsc = kept("bsc", [P, F], U8)
        b_codes = {(w, c): kept("b_codes%d%d" % (w, c), [P, CHUNK], U32) for w in range(2) for c in range(CHUNKS)}
        x_codes = [kept("x_codes%d" % k, [P, 2 * PASSES * P], U32) for k in range(TILES // 2)]
        x_sc = [kept("x_sc%d" % k, [P, 2 * PASSES * P], U8) for k in range(TILES // 2)]
        w_codes = [kept("w_codes%d" % q, [P, CHUNK], U32) for q in range(CHUNKS * PASSES)]
        w_sc = [kept("w_sc%d" % q, [P, CHUNK], U8) for q in range(CHUNKS * PASSES)]

        def load_x(k):
            nc.sync.dma_start(out=x_raw[k][:], in_=x_bytes[512 * k : 512 * (k + 1), :].rearrange("(i p) d -> p i d", p=P))

        def load_a(w, g):
            src = a_words[w][0].rearrange("p n t -> p (n t)")[:, 2048 * g : 2048 * (g + 1)].bitcast(I32)
            nc.sync.dma_start(out=a_raw[w, g][:].bitcast(I32), in_=src)

        def load_b(w, c):
            src = b_words[w][0].rearrange("p n t -> p (n t)")[:, 2048 * c : 2048 * (c + 1)].bitcast(I32)
            nc.sync.dma_start(out=b_codes[w, c][:].bitcast(I32), in_=src)

        def load_asc(w, quads, queue):
            for q in quads:
                src = a_scales[w][0, 4 * q : 4 * q + 4, :].bitcast(I32).rearrange("r (g n) -> g r n", g=PASSES)
                row = 32 * q + 8 * w
                queue.dma_start(out=asc_raw[row : row + 8, :].bitcast(I32), in_=src)

        def load_bsc(w, quads, queue):
            for q in quads:
                row = 32 * q + 4 + 4 * w
                queue.dma_start(out=bsc[row : row + 4, :].bitcast(I32), in_=b_scales[w][0, 4 * q : 4 * q + 4, :].bitcast(I32))

        nc.vector.memset(asc_raw[:].bitcast(I32), 0)
        nc.vector.memset(bsc[:].bitcast(I32), 0)
        nc.vector.memset(bias_rows[:].bitcast(I32), 0)
        make_identity(nc, ident[:])
        load_asc(0, range(NA, 4), nc.gpsimd)
        load_bsc(0, range(NB), nc.gpsimd)
        nc.scalar.activation(out=sel[:], in_=ident[:, 0:CHUNKS], func=ACT.Square)

        nc.sync.dma_start(out=xs_all[:], in_=x_scale.rearrange("i j -> (i j)").partition_broadcast(P))
        load_x(0)
        if X_FIRST:
            load_x(1)
        load_asc(1, range(4), nc.sync)
        load_asc(0, range(NA), nc.sync)
        load_a(1, 0)
        load_a(0, 0)
        load_b(1, 0)
        load_bsc(1, range(4), nc.sync)
        load_b(0, 0)
        load_bsc(0, range(NB, 4), nc.sync)
        if not X_FIRST:
            load_x(1)
        load_a(1, 1)
        load_a(0, 1)
        nc.sync.dma_start(out=bias_rows[0:CHUNKS, :], in_=bias.rearrange("(c n) -> c n", n=CHUNK))
        for c in range(1, CHUNKS):
            load_b(1, c)
            load_b(0, c)

        x_wide, x_banks, x_turned = {}, {}, {}
        w2_sb, w1_banks, w_bf, h_banks, s_pairs, r_pairs = {}, {}, {}, {}, {}, {}

        def widen(i, on_vector, blocks):
            if i not in x_wide:
                x_wide[i] = work.tile([P, D], BF16, name="x_wide", align_bytes=64, bufs=8)
            for j in blocks:
                cols = slice(P * j, P * (j + 1))
                src = x_raw[i // 4][:, i % 4, cols].bitcast(FP8)
                scale = xs_all[:, TILES * i + j : TILES * i + j + 1]
                if on_vector:
                    nc.vector.tensor_scalar(out=x_wide[i][:, cols], in0=src, scalar1=scale, scalar2=None, op0=ALU.mult)
                else:
                    nc.scalar.activation(out=x_wide[i][:, cols], in_=src, func=ACT.Copy, scale=scale)

        def turn(i, tag):
            x_banks[i] = psum.tile([P, PASSES, 2, P], F32, name="x_bank", tag=tag, bufs=BANKS[tag])
            words = x_wide[i][:].bitcast(F32)
            for g in range(PASSES):
                for u in range(2):
                    nc.tensor.transpose(x_banks[i][:, g, u, :], words[:, 256 * g + u : 256 * (g + 1) : 2], ident[:])

        def empty_x(i):
            k = i // 2
            if k not in x_turned:
                x_turned[k] = work.tile([P, 2, PASSES * P * 2], F32, name="x_turned", align_bytes=64, bufs=4)
            nc.scalar.copy(
                out=x_turned[k][:, i % 2, :].rearrange("p (g n u) -> p g n u", g=PASSES, u=2),
                in_=x_banks[i][:].rearrange("p g u n -> p g n u"),
            )

        def quantize_x(k):
            nc.vector.quantize_mx(
                out=x_codes[k][:].bitcast(FP8X4), scales=x_sc[k][:],
                in_=x_turned[k][:].rearrange("p i n -> p (i n)").bitcast(BF16),
            )

        def permute_a(w, g):
            (nc.gpsimd if g and PERM_POOL else nc.vector).tensor_copy(
                out=a_codes[w, g][:].bitcast(I32).rearrange("p (t b i) -> p b t i", t=PACK, i=4),
                in_=a_raw[w, g][:].bitcast(I32).rearrange("p (b i t) -> p b t i", t=PACK, i=4),
            )

        def permute_asc():
            nc.vector.tensor_copy(
                out=asc[:].rearrange("p (t m) -> p t m", t=PACK),
                in_=asc_raw[:].rearrange("p (m t) -> p t m", t=PACK),
            )

        def spread_bias(half):
            bank = psum.tile([P, 2 * CHUNK], BF16, name="bias_bank", tag="h")
            for e in range(2):
                c = 2 * half + e
                nc.tensor.matmul(
                    bank[:, CHUNK * e : CHUNK * (e + 1)], lhsT=sel[:, c : c + 1].to_broadcast([P, P]),
                    rhs=bias_rows[:], start=True, stop=True,
                )
            nc.scalar.copy(out=bias_all[:, 2 * CHUNK * half : 2 * CHUNK * (half + 1)], in_=bank[:])

        def factor_product(w, u, bank):
            c, g, s = u // (PASSES * SUBS), u // SUBS % PASSES, u % SUBS
            a_row, b_row = 8 * w + 4 * g, 4 + 4 * w
            for t in range(PACK):
                nc.tensor.matmul_mx(
                    out=bank[:, t, :],
                    lhsT=a_codes[w, g][:, P * t : P * (t + 1)].bitcast(FP8X4),
                    lhsT_scale=asc[a_row:P, P * t : P * (t + 1)],
                    rhs=b_codes[w, c][:, P * s : P * (s + 1)].bitcast(FP8X4),
                    rhs_scale=bsc[b_row:P, CHUNK * c + P * s : CHUNK * c + P * (s + 1)],
                    start=True, stop=True,
                )

        def w_products(u):
            w2_bank = psum.tile([P, PACK, P], F32, name="w2_bank", tag="w2", bufs=2)
            factor_product(1, u, w2_bank)
            w1_banks[u] = psum.tile([P, PACK, P], F32, name="w1_bank", tag="w1")
            factor_product(0, u, w1_banks[u])
            w2_sb[u] = work.tile([P, P, PACK], F32, name="w2_sb", align_bytes=64)
            nc.scalar.copy(out=w2_sb[u][:], in_=w2_bank[:].rearrange("p t n -> p n t"))

        def w_combine(u):
            q, s = u // SUBS, u % SUBS
            if s == 0:
                w_bf[q] = work.tile([P, CHUNK, PACK], BF16, name="w_bf", align_bytes=64)
            nc.vector.scalar_tensor_tensor(
                out=w_bf[q][:, P * s : P * (s + 1), :], in0=w2_sb[u][:], scalar=1.0,
                in1=w1_banks[u][:].rearrange("p t n -> p n t"), op0=ALU.add, op1=ALU.mult,
            )

        def quantize_w(q):
            nc.vector.quantize_mx(
                out=w_codes[q][:].bitcast(FP8X4), scales=w_sc[q][:], in_=w_bf[q][:].rearrange("p n t -> p (n t)"),
            )

        def h_product(v):
            c, i = v // TILES, v % TILES
            tag = "w1" if v > W_UNITS - H_LAG and v % 2 == 0 else "h"
            h_banks[v] = psum.tile([P, CHUNK], F32, name="h_bank", tag=tag)
            for g in range(PASSES):
                cols = slice(P * (PASSES * (i % 2) + g), P * (PASSES * (i % 2) + g + 1))
                nc.tensor.matmul_mx(
                    out=h_banks[v][:],
                    lhsT=x_codes[i // 2][:, cols].bitcast(FP8X4), lhsT_scale=x_sc[i // 2][:, cols],
                    rhs=w_codes[PASSES * c + g][:].bitcast(FP8X4), rhs_scale=w_sc[PASSES * c + g][:],
                    start=(g == 0), stop=(g == PASSES - 1),
                )

        def add_bias(v):
            c = v // TILES
            if v % 2 == 0:
                s_pairs[v // 2] = work.tile([P, 2, CHUNK], F32, name="s_pair", align_bytes=64, bufs=5)
            nc.vector.tensor_tensor(
                out=s_pairs[v // 2][:, v % 2, :], in0=h_banks[v][:],
                in1=bias_all[:, CHUNK * c : CHUNK * (c + 1)], op=ALU.add,
            )

        def relu_pair(k):
            r_pairs[k] = work.tile([P, 2, CHUNK], F32, name="r_pair", align_bytes=64, bufs=5)
            if k in ACT_PAIRS:
                for e in range(2):
                    nc.scalar.activation(out=r_pairs[k][:, e, :], in_=s_pairs[k][:, e, :], func=ACT.Relu)
                for e in range(2):
                    square(2 * k + e)
                return
            nc.gpsimd.tensor_scalar(out=r_pairs[k][:], in0=s_pairs[k][:], scalar1=F32_MAX, scalar2=0.0, op0=ALU.min, op1=ALU.max)

        def store(v, res):
            c, i = v // TILES, v % TILES
            nc.sync.dma_start(out=out[P * i : P * (i + 1), CHUNK * c : CHUNK * (c + 1)], in_=res[:])

        def square(v):
            res = work.tile([P, CHUNK], F32, name="res", align_bytes=64, bufs=12)
            r = r_pairs[v // 2][:, v % 2, :]
            if v in POOL_SQ:
                nc.gpsimd.tensor_tensor(out=res[:], in0=r, in1=r, op=ALU.mult)
            else:
                nc.scalar.activation(out=res[:], in_=r, func=ACT.Square)
            store(v, res)

        def relu_square(v):
            res = work.tile([P, CHUNK], F32, name="res", align_bytes=64, bufs=12)
            s = s_pairs[v // 2][:, v % 2, :]
            nc.vector.scalar_tensor_tensor(out=res[:], in0=s, scalar=0.0, in1=s, op0=ALU.max, op1=ALU.mult)
            store(v, res)

        warm_bank = psum.tile([P, P], F32, name="warm_bank", tag="w1")

        def warm(count):
            for k in range(count * WARM):
                nc.tensor.matmul(warm_bank[:], lhsT=ident[:], rhs=ident[:], start=True, stop=True)

        last = W_UNITS - 1
        state = {"done": 0}

        def front(m):
            if m < last:
                w_products(m)
            v = m - H_LAG
            if 0 <= v < H_UNITS:
                h_product(v)

        def back(m):
            v = m - H_LAG
            if m < last:
                w_combine(m)
            if m == last - 1:
                w_products(last)
                w_combine(last)
            if m % SUBS == 1 and 0 <= m // SUBS - 1 < CHUNKS * PASSES - 1:
                quantize_w(m // SUBS - 1)
            if m == last:
                quantize_w(CHUNKS * PASSES - 1)
            if 0 <= v < H_UNITS:
                add_bias(v)
            lag = SQ_LAG if m < last else TAIL_LAG
            while state["done"] < POOL_UNITS and state["done"] <= m - lag:
                if state["done"] // 2 not in ACT_PAIRS:
                    square(state["done"])
                state["done"] += 1
            if 0 <= v < POOL_UNITS and v % 2 == 1:
                relu_pair(v // 2)

        calls = {
            "wv": lambda i, h: widen(i, True, range(4 * h, 4 * h + 4)),
            "wa": lambda i, h: widen(i, False, range(4 * h, 4 * h + 4)),
            "t": turn, "e": empty_x, "q": quantize_x, "pa": permute_a, "ps": permute_asc,
            "warm": warm, "bias": spread_bias, "F": front, "B": back,
        }
        for job in ORDER:
            calls[job[0]](*job[1:])
        for m in range(20, H_UNITS + SQ_LAG):
            front(m)
            back(m)
        for v in range(POOL_UNITS, H_UNITS):
            relu_square(v)
